import numpy as np
import ml_dtypes


def mxq(x, axis, fmt="e4m3"):
    dtype, down = {"e4m3": (ml_dtypes.float8_e4m3fn, 7), "e5m2": (ml_dtypes.float8_e5m2, 14)}[fmt]
    v = np.moveaxis(np.asarray(x, np.float32).astype(ml_dtypes.bfloat16).astype(np.float64), axis, -1)
    blocks = v.reshape(v.shape[:-1] + (-1, 32))
    amax = np.abs(blocks).max(-1, keepdims=True)
    byte = np.maximum(np.where(amax > 0, np.frexp(amax)[1] - 1 + 127, 0) - down, 1)
    scale = np.exp2(byte - 127.0)
    codes = (blocks / scale).astype(np.float32).astype(dtype).astype(np.float64)
    return np.moveaxis((codes * scale).reshape(v.shape), -1, axis)


WIDE = False


def mx_kscale(k):
    if not WIDE:
        return np.ones(k)
    levels = np.array([10, -10, 5, -5, 0])
    if k % 512:
        return np.exp2(np.random.permutation(np.resize(levels, k // 32))).repeat(32)
    a = np.empty((k // 512, 16))
    for p in range(k // 512):
        a[p, :8] = np.random.permutation(np.resize(levels, 8))
        for g in range(8):
            far = levels[np.abs(levels - a[p, g]) >= 10]
            a[p, g + 8] = far[np.random.randint(len(far))]
    return np.exp2(a.ravel()).repeat(32)


def f64(x):
    return np.asarray(x).astype(np.float64)


def striped(idx):
    return np.tile(idx.reshape(-1, 16).T, (8, 1)).astype(np.uint16)


def unstriped(offs):
    return offs[:16].T.reshape(-1).astype(np.int64)


E2M1 = np.array([0.0, 0.5, 1.0, 1.5, 2.0, 3.0, 4.0, 6.0, -0.0, -0.5, -1.0, -1.5, -2.0, -3.0, -4.0, -6.0])


def pack_weight(w, fmt):
    k, n = w.shape
    w = f64(np.asarray(w, np.float32).astype(ml_dtypes.bfloat16)).reshape(k // 32, 32, n)
    amax = np.abs(w).max(1)
    if fmt == "e4m3":
        byte = np.frexp(amax)[1] - 1 + 127 - 7
    else:
        mant, ex = np.frexp(amax / 6.0)
        byte = np.where(mant > 0.5, ex, ex - 1) + 127
    byte = np.clip(np.where(amax > 0, byte, 1), 1, 254)
    scaled = (w * np.exp2(127.0 - byte)[:, None, :]).reshape(k, n).astype(np.float32)
    by_word = np.ascontiguousarray(scaled.reshape(k // 512, 128, 4, n).transpose(0, 1, 3, 2))
    if fmt == "e4m3":
        words = by_word.astype(ml_dtypes.float8_e4m3fn).view(np.uint8)
    else:
        c = by_word.astype(ml_dtypes.float4_e2m1fn).view(np.uint8) & 0xF
        words = (c[..., 0::2] | (c[..., 1::2] << 4)).reshape(k // 512, 128, 2 * n)
    return np.ascontiguousarray(words), np.ascontiguousarray(byte.astype(np.uint8).reshape(k // 512, 16, n))


def unpack_weight(words, scales, fmt):
    g, _, n = scales.shape
    words = np.ascontiguousarray(words).reshape(g, 128, n, -1)
    if fmt == "e4m3":
        vals = words.view(ml_dtypes.float8_e4m3fn).astype(np.float64)
    else:
        nib = np.empty((g, 128, n, 4), np.uint8)
        nib[..., 0::2] = words & 0xF
        nib[..., 1::2] = words >> 4
        vals = E2M1[nib]
    vals = vals * np.repeat(np.exp2(scales.astype(np.float64) - 127.0), 8, axis=1)[..., None]
    return vals.transpose(0, 1, 3, 2).reshape(g * 512, n)


K, T, E, C, N = 256, 1280, 8, 128, 512


def by_expert(wq, xq):
    return np.concatenate([wq[e].T @ xq[:, e * C:(e + 1) * C] for e in range(E)], axis=1)


def setup_inputs():
    n = np.random.standard_normal
    s = mx_kscale(N)[:, None]
    w = [pack_weight(m, "e2m1") for m in n((E + 1, N, K)) / np.sqrt(N) / s[None]]
    return {
        "dyT": (n((N, T)) * s).astype(np.float32),
        "w_words": np.stack([m[0] for m in w]),
        "w_scales": np.stack([m[1] for m in w]),
        "gate": np.tile(np.random.uniform(0.2, 1.0, E * C), (N, 1)).astype(np.float32),
        "offs": striped(np.random.permutation(T)[:E * C]),
    }


def reference(dyT, w_words, w_scales, gate, offs):
    idx = unstriped(offs)
    w = np.stack([unpack_weight(w_words[e], w_scales[e], "e2m1") for e in range(E + 1)])
    gq = mxq(f64(gate) * f64(dyT)[:, idx], 0, "e4m3")
    wq = w
    ds = wq[E].T @ mxq(f64(dyT), 0, "e4m3")
    dx = by_expert(wq, gq)
    ds[:, idx] += dx
    return ds

@@ -1,0 +1,154 @@
+from contextlib import ExitStack
+
+import concourse.mybir as mybir
+
+K, T, E, C, N = 256, 1280, 8, 128, 512
+SLOTS = E * C
+FLOPS = 2 * N * K * (SLOTS + T)
+BYTES = 4 * N * T + (E + 1) * (N * K // 2 + N * K // 32) + 4 * SLOTS + 2 * SLOTS + 4 * K * T
+
+F32 = mybir.dt.float32
+BF16 = mybir.dt.bfloat16
+I32 = mybir.dt.int32
+U32 = mybir.dt.uint32
+U16 = mybir.dt.uint16
+U8 = mybir.dt.uint8
+FP8X4 = mybir.dt.float8_e4m3fn_x4
+FP4X4 = mybir.dt.float4_e2m1fn_x4
+MULT = mybir.AluOpType.mult
+ADD = mybir.AluOpType.add
+
+P = 128
+PACK = 4
+KB = K // P
+GROUP = 256
+GROUPS = SLOTS // GROUP
+GATE_HEAD = 384
+EARLY_EXPERTS = 4
+TOKEN_CHUNKS = [(0, 512), (512, 1024), (1024, 1280)]
+COPY_TOKENS = 256
+
+
+def tile_moe_bds_lin_none_kernel(tc, dyT, w_words, w_scales, gate, offs, out):
+    nc = tc.nc
+
+    with ExitStack() as ctx:
+        keep = ctx.enter_context(tc.tile_pool(name="keep", bufs=1))
+        dx_psum = ctx.enter_context(tc.psum_pool(name="dx_psum", bufs=3))
+        ds_psum = ctx.enter_context(tc.psum_pool(name="ds_psum", bufs=1))
+
+        offsets = keep.tile([P, SLOTS // 16], U16, name="offsets")
+        rows = [keep.tile([P, T], F32, name="rows%d" % t) for t in range(PACK)]
+        gates = keep.tile([P, SLOTS], F32, name="gates")
+        words = keep.tile([P, E + 1, 2 * K], U8, name="words", align_bytes=64)
+        planes = keep.tile([P, E + 1, K], U8, name="planes", align_bytes=64)
+        tokens = [keep.tile([P, PACK, b - a], F32, name="tokens%d" % a) for a, b in TOKEN_CHUNKS]
+        windows = [keep.tile([P, T], F32, name="window%d" % kb) for kb in range(KB)]
+        g_rows = keep.tile([P, PACK, SLOTS], F32, name="g_rows")
+        g_bf = keep.tile([P, SLOTS, PACK], BF16, name="g_bf", align_bytes=64)
+        g_codes = keep.tile([P, SLOTS], U32, name="g_codes", align_bytes=64)
+        g_scales = keep.tile([P, SLOTS], U8, name="g_scales", align_bytes=64)
+        y_bf = keep.tile([P, T, PACK], BF16, name="y_bf", align_bytes=64)
+        y_codes = keep.tile([P, T], U32, name="y_codes", align_bytes=64)
+        y_scales = keep.tile([P, T], U8, name="y_scales", align_bytes=64)
+        dx = keep.tile([P, KB, SLOTS], F32, name="dx")
+        result = keep.tile([P, KB, T], F32, name="result")
+
+        dy_rows = dyT.rearrange("(p t) c -> p t c", t=PACK)
+
+        nc.vector.memset(planes[:].bitcast(I32), 0)
+        for kb in range(KB):
+            nc.vector.memset(windows[kb][:], 0.0)
+
+        def load_words(first, last):
+            nc.sync.dma_start(
+                out=words[:, first:last, :].bitcast(I32),
+                in_=w_words[first:last, 0].rearrange("e p b -> p e b").bitcast(I32),
+            )
+
+        nc.sync.dma_start(offsets[:], offs)
+        nc.sync.dma_start(out=gates[:, 0:GATE_HEAD], in_=gate[0:P, 0:GATE_HEAD])
+        nc.sync.dma_start(out=rows[0][:], in_=dy_rows[:, 0, :])
+        nc.sync.dma_start(out=gates[:, GATE_HEAD:SLOTS], in_=gate[0:P, GATE_HEAD:SLOTS])
+        for t in range(1, PACK):
+            nc.sync.dma_start(out=rows[t][:], in_=dy_rows[:, t, :])
+        load_words(0, EARLY_EXPERTS)
+        for r in range(4):
+            nc.sync.dma_start(
+                out=planes[r:P:32, :, :].bitcast(I32),
+                in_=w_scales[:, 0, r:16:4, :].rearrange("e q k -> q e k").bitcast(I32),
+            )
+        load_words(EARLY_EXPERTS, E + 1)
+        for i, (a, b) in enumerate(TOKEN_CHUNKS):
+            nc.sync.dma_start(out=tokens[i][:], in_=dy_rows[:, :, a:b])
+
+        def gather(t, a, b):
+            nc.vector.tensor_tensor(
+                g_rows[:, t, a:b], rows[t][:].indirect(offsets[:, a // 16 : b // 16]), gates[:, a:b], MULT
+            )
+
+        def interleave(dst, src):
+            nc.scalar.copy(
+                out=dst.rearrange("p (c i) t -> p c t i", i=4),
+                in_=src.rearrange("p t (c i) -> p c t i", i=4),
+            )
+
+        def quantize(codes, scales, values):
+            nc.vector.quantize_mx(out=codes.bitcast(FP8X4), scales=scales, in_=values.rearrange("p c t -> p (c t)"))
+
+        def product(acc, e, kb, codes, scales):
+            nc.tensor.matmul_mx(
+                out=acc,
+                lhsT=words[:, e, 2 * P * kb : 2 * P * (kb + 1)].bitcast(FP4X4),
+                lhsT_scale=planes[:, e, P * kb : P * (kb + 1)],
+                rhs=codes.bitcast(FP8X4),
+                rhs_scale=scales,
+                start=True,
+                stop=True,
+            )
+
+        def experts(q):
+            a, b = q * GROUP, (q + 1) * GROUP
+            quantize(g_codes[:, a:b], g_scales[:, a:b], g_bf[:, a:b, :])
+            bank = dx_psum.tile([P, KB, GROUP], F32, name="dx_bank")
+            for kb in range(KB):
+                for c0 in range(0, GROUP, C):
+                    e = (a + c0) // C
+                    product(bank[:, kb, c0 : c0 + C], e, kb, g_codes[:, e * C : (e + 1) * C], g_scales[:, e * C : (e + 1) * C])
+            nc.scalar.copy(out=dx[:, :, a:b], in_=bank[:])
+
+        gather(0, 0, GATE_HEAD)
+        gather(0, GATE_HEAD, SLOTS)
+        gather(1, 0, SLOTS)
+        for q in range(GROUPS):
+            a, b = q * GROUP, (q + 1) * GROUP
+            gather(2, a, b)
+            gather(3, a, b)
+            interleave(g_bf[:, a:b, :], g_rows[:, :, a:b])
+            if q > 0:
+                experts(q - 1)
+        experts(GROUPS - 1)
+
+        def scatter(kb):
+            for q in range(GROUPS):
+                a, b = q * GROUP, (q + 1) * GROUP
+                nc.vector.tensor_copy(windows[kb][:].indirect(offsets[:, a // 16 : b // 16]), dx[:, kb, a:b])
+
+        tail_bank = ds_psum.tile([P, KB, 256], F32, name="tail_bank")
+        ds = {}
+        for i, (a, b) in enumerate(TOKEN_CHUNKS):
+            for c0 in range(0, b - a, COPY_TOKENS):
+                interleave(y_bf[:, a + c0 : a + c0 + COPY_TOKENS, :], tokens[i][:, :, c0 : c0 + COPY_TOKENS])
+            quantize(y_codes[:, a:b], y_scales[:, a:b], y_bf[:, a:b, :])
+            for kb in range(KB):
+                if b - a == 512:
+                    ds[kb, i] = ds_psum.tile([P, 512], F32, name="ds%d_%d" % (kb, i))[:]
+                else:
+                    ds[kb, i] = tail_bank[:, kb, :]
+                product(ds[kb, i], E, kb, y_codes[:, a:b], y_scales[:, a:b])
+
+        for kb in range(KB):
+            scatter(kb)
+            for i, (a, b) in enumerate(TOKEN_CHUNKS):
+                nc.vector.tensor_tensor(result[:, kb, a:b], ds[kb, i], windows[kb][:, a:b], ADD)
+                nc.sync.dma_start(out=out[kb * P : (kb + 1) * P, a:b], in_=result[:, kb, a:b])

@@ -21,11 +21,11 @@ ADD = mybir.AluOpType.add
 P = 128
 PACK = 4
 KB = K // P
-GROUP = 256
-GROUPS = SLOTS // GROUP
-GATE_HEAD = 384
-EARLY_EXPERTS = 4
-TOKEN_CHUNKS = [(0, 512), (512, 1024), (1024, 1280)]
+BANK = 512
+FIRST, MIDDLE, LAST = (0, 256), (256, 768), (768, 1024)
+EARLY_EXPERTS = 2
+TOKEN_LOADS = [(0, 256), (256, 768), (768, 1280)]
+TOKEN_BANKS = [(0, 512), (512, 1024), (1024, 1280)]
 COPY_TOKENS = 256
 
 
@@ -34,31 +34,29 @@ def tile_moe_bds_lin_none_kernel(tc, dyT, w_words, w_scales, gate, offs, out):
 
     with ExitStack() as ctx:
         keep = ctx.enter_context(tc.tile_pool(name="keep", bufs=1))
-        dx_psum = ctx.enter_context(tc.psum_pool(name="dx_psum", bufs=3))
-        ds_psum = ctx.enter_context(tc.psum_pool(name="ds_psum", bufs=1))
+        psum = ctx.enter_context(tc.psum_pool(name="psum", bufs=1))
 
         offsets = keep.tile([P, SLOTS // 16], U16, name="offsets")
         rows = [keep.tile([P, T], F32, name="rows%d" % t) for t in range(PACK)]
         gates = keep.tile([P, SLOTS], F32, name="gates")
         words = keep.tile([P, E + 1, 2 * K], U8, name="words", align_bytes=64)
         planes = keep.tile([P, E + 1, K], U8, name="planes", align_bytes=64)
-        tokens = [keep.tile([P, PACK, b - a], F32, name="tokens%d" % a) for a, b in TOKEN_CHUNKS]
+        tokens = [keep.tile([P, PACK, b - a], F32, name="tokens%d" % a) for a, b in TOKEN_LOADS]
         windows = [keep.tile([P, T], F32, name="window%d" % kb) for kb in range(KB)]
-        g_rows = keep.tile([P, PACK, SLOTS], F32, name="g_rows")
         g_bf = keep.tile([P, SLOTS, PACK], BF16, name="g_bf", align_bytes=64)
         g_codes = keep.tile([P, SLOTS], U32, name="g_codes", align_bytes=64)
         g_scales = keep.tile([P, SLOTS], U8, name="g_scales", align_bytes=64)
         y_bf = keep.tile([P, T, PACK], BF16, name="y_bf", align_bytes=64)
         y_codes = keep.tile([P, T], U32, name="y_codes", align_bytes=64)
         y_scales = keep.tile([P, T], U8, name="y_scales", align_bytes=64)
-        dx = keep.tile([P, KB, SLOTS], F32, name="dx")
+        dx = keep.tile([P, KB, MIDDLE[1]], F32, name="dx")
         result = keep.tile([P, KB, T], F32, name="result")
 
         dy_rows = dyT.rearrange("(p t) c -> p t c", t=PACK)
 
         nc.vector.memset(planes[:].bitcast(I32), 0)
-        for kb in range(KB):
-            nc.vector.memset(windows[kb][:], 0.0)
+        nc.vector.memset(windows[0][:], 0.0)
+        nc.gpsimd.memset(windows[1][:], 0.0)
 
         def load_words(first, last):
             nc.sync.dma_start(
@@ -66,12 +64,16 @@ def tile_moe_bds_lin_none_kernel(tc, dyT, w_words, w_scales, gate, offs, out):
                 in_=w_words[first:last, 0].rearrange("e p b -> p e b").bitcast(I32),
             )
 
+        def load_gate(a, b):
+            nc.sync.dma_start(out=gates[:, a:b], in_=gate[0:P, a:b])
+
         nc.sync.dma_start(offsets[:], offs)
-        nc.sync.dma_start(out=gates[:, 0:GATE_HEAD], in_=gate[0:P, 0:GATE_HEAD])
+        load_gate(*FIRST)
         nc.sync.dma_start(out=rows[0][:], in_=dy_rows[:, 0, :])
-        nc.sync.dma_start(out=gates[:, GATE_HEAD:SLOTS], in_=gate[0:P, GATE_HEAD:SLOTS])
+        load_gate(*MIDDLE)
         for t in range(1, PACK):
             nc.sync.dma_start(out=rows[t][:], in_=dy_rows[:, t, :])
+        load_gate(*LAST)
         load_words(0, EARLY_EXPERTS)
         for r in range(4):
             nc.sync.dma_start(
@@ -79,12 +81,12 @@ def tile_moe_bds_lin_none_kernel(tc, dyT, w_words, w_scales, gate, offs, out):
                 in_=w_scales[:, 0, r:16:4, :].rearrange("e q k -> q e k").bitcast(I32),
             )
         load_words(EARLY_EXPERTS, E + 1)
-        for i, (a, b) in enumerate(TOKEN_CHUNKS):
+        for i, (a, b) in enumerate(TOKEN_LOADS):
             nc.sync.dma_start(out=tokens[i][:], in_=dy_rows[:, :, a:b])
 
-        def gather(t, a, b):
+        def gather(g_rows, t, a, b):
             nc.vector.tensor_tensor(
-                g_rows[:, t, a:b], rows[t][:].indirect(offsets[:, a // 16 : b // 16]), gates[:, a:b], MULT
+                g_rows[:, t, :], rows[t][:].indirect(offsets[:, a // 16 : b // 16]), gates[:, a:b], MULT
             )
 
         def interleave(dst, src):
@@ -107,48 +109,64 @@ def tile_moe_bds_lin_none_kernel(tc, dyT, w_words, w_scales, gate, offs, out):
                 stop=True,
             )
 
-        def experts(q):
-            a, b = q * GROUP, (q + 1) * GROUP
+        def experts(sums, a, b):
             quantize(g_codes[:, a:b], g_scales[:, a:b], g_bf[:, a:b, :])
-            bank = dx_psum.tile([P, KB, GROUP], F32, name="dx_bank")
             for kb in range(KB):
-                for c0 in range(0, GROUP, C):
-                    e = (a + c0) // C
-                    product(bank[:, kb, c0 : c0 + C], e, kb, g_codes[:, e * C : (e + 1) * C], g_scales[:, e * C : (e + 1) * C])
-            nc.scalar.copy(out=dx[:, :, a:b], in_=bank[:])
+                for c0 in range(a, b, C):
+                    product(sums[kb][:, c0 - a : c0 - a + C], c0 // C, kb, g_codes[:, c0 : c0 + C], g_scales[:, c0 : c0 + C])
 
-        gather(0, 0, GATE_HEAD)
-        gather(0, GATE_HEAD, SLOTS)
-        gather(1, 0, SLOTS)
-        for q in range(GROUPS):
-            a, b = q * GROUP, (q + 1) * GROUP
-            gather(2, a, b)
-            gather(3, a, b)
-            interleave(g_bf[:, a:b, :], g_rows[:, :, a:b])
-            if q > 0:
-                experts(q - 1)
-        experts(GROUPS - 1)
+        def scatter(kb, values, a, b):
+            nc.vector.tensor_copy(windows[kb][:].indirect(offsets[:, a // 16 : b // 16]), values)
 
-        def scatter(kb):
-            for q in range(GROUPS):
-                a, b = q * GROUP, (q + 1) * GROUP
-                nc.vector.tensor_copy(windows[kb][:].indirect(offsets[:, a // 16 : b // 16]), dx[:, kb, a:b])
+        def combine(kb):
+            for i, (a, b) in enumerate(TOKEN_BANKS):
+                nc.vector.tensor_tensor(result[:, kb, a:b], ds[kb, i], windows[kb][:, a:b], ADD)
+                nc.sync.dma_start(out=out[kb * P : (kb + 1) * P, a:b], in_=result[:, kb, a:b])
 
-        tail_bank = ds_psum.tile([P, KB, 256], F32, name="tail_bank")
+        g_first = keep.tile([P, PACK, FIRST[1] - FIRST[0]], F32, name="g_edge")
+        g_middle = keep.tile([P, PACK, MIDDLE[1] - MIDDLE[0]], F32, name="g_middle")
+        for t in range(PACK):
+            gather(g_first, t, *FIRST)
+            gather(g_middle, t, *MIDDLE)
+        interleave(g_bf[:, FIRST[0] : FIRST[1], :], g_first[:])
+        interleave(g_bf[:, MIDDLE[0] : MIDDLE[1], :], g_middle[:])
+
+        first_bank = psum.tile([P, KB, FIRST[1] - FIRST[0]], F32, name="pair_bank")
+        experts([first_bank[:, kb, :] for kb in range(KB)], *FIRST)
+        nc.scalar.copy(out=dx[:, :, FIRST[0] : FIRST[1]], in_=first_bank[:])
+
+        g_last = keep.tile([P, PACK, LAST[1] - LAST[0]], F32, name="g_edge")
+        for t in range(PACK):
+            gather(g_last, t, *LAST)
+        interleave(g_bf[:, LAST[0] : LAST[1], :], g_last[:])
+
+        middle_banks = [psum.tile([P, BANK], F32, name="middle_bank%d" % kb) for kb in range(KB)]
+        experts([bank[:] for bank in middle_banks], *MIDDLE)
+        for kb in range(KB):
+            scatter(kb, dx[:, kb, FIRST[0] : FIRST[1]], *FIRST)
+        last_bank = psum.tile([P, KB, LAST[1] - LAST[0]], F32, name="last_bank")
+        experts([last_bank[:, kb, :] for kb in range(KB)], *LAST)
+        for kb in range(KB):
+            nc.scalar.copy(out=dx[:, kb, MIDDLE[0] : MIDDLE[1]], in_=middle_banks[kb][:])
+            scatter(kb, dx[:, kb, MIDDLE[0] : MIDDLE[1]], *MIDDLE)
+
+        tail_bank = psum.tile([P, KB, TOKEN_BANKS[2][1] - TOKEN_BANKS[2][0]], F32, name="pair_bank")
         ds = {}
-        for i, (a, b) in enumerate(TOKEN_CHUNKS):
-            for c0 in range(0, b - a, COPY_TOKENS):
-                interleave(y_bf[:, a + c0 : a + c0 + COPY_TOKENS, :], tokens[i][:, :, c0 : c0 + COPY_TOKENS])
+        for i, (a, b) in enumerate(TOKEN_BANKS):
+            for c0 in range(a, b, COPY_TOKENS):
+                j = [lo <= c0 < hi for lo, hi in TOKEN_LOADS].index(True)
+                lo = c0 - TOKEN_LOADS[j][0]
+                interleave(y_bf[:, c0 : c0 + COPY_TOKENS, :], tokens[j][:, :, lo : lo + COPY_TOKENS])
             quantize(y_codes[:, a:b], y_scales[:, a:b], y_bf[:, a:b, :])
             for kb in range(KB):
-                if b - a == 512:
-                    ds[kb, i] = ds_psum.tile([P, 512], F32, name="ds%d_%d" % (kb, i))[:]
+                if b - a == BANK:
+                    ds[kb, i] = psum.tile([P, BANK], F32, name="ds%d_%d" % (kb, i))[:]
                 else:
                     ds[kb, i] = tail_bank[:, kb, :]
                 product(ds[kb, i], E, kb, y_codes[:, a:b], y_scales[:, a:b])
 
+        dx_last = keep.tile([P, KB, LAST[1] - LAST[0]], F32, name="tokens%d" % TOKEN_LOADS[-1][0])
         for kb in range(KB):
-            scatter(kb)
-            for i, (a, b) in enumerate(TOKEN_CHUNKS):
-                nc.vector.tensor_tensor(result[:, kb, a:b], ds[kb, i], windows[kb][:, a:b], ADD)
-                nc.sync.dma_start(out=out[kb * P : (kb + 1) * P, a:b], in_=result[:, kb, a:b])
+            nc.scalar.copy(out=dx_last[:, kb, :], in_=last_bank[:, kb, :])
+            scatter(kb, dx_last[:, kb, :], *LAST)
+            combine(kb)

@@ -23,6 +23,7 @@ PACK = 4
 KB = K // P
 BANK = 512
 FIRST, MIDDLE, LAST = (0, 256), (256, 768), (768, 1024)
+HELD = (512, 768)
 EARLY_EXPERTS = 2
 TOKEN_LOADS = [(0, 256), (256, 768), (768, 1280)]
 TOKEN_BANKS = [(0, 512), (512, 1024), (1024, 1280)]
@@ -118,10 +119,10 @@ def tile_moe_bds_lin_none_kernel(tc, dyT, w_words, w_scales, gate, offs, out):
         def scatter(kb, values, a, b):
             nc.vector.tensor_copy(windows[kb][:].indirect(offsets[:, a // 16 : b // 16]), values)
 
-        def combine(kb):
+        def combine(engine, queue, kb):
             for i, (a, b) in enumerate(TOKEN_BANKS):
-                nc.vector.tensor_tensor(result[:, kb, a:b], ds[kb, i], windows[kb][:, a:b], ADD)
-                nc.sync.dma_start(out=out[kb * P : (kb + 1) * P, a:b], in_=result[:, kb, a:b])
+                engine.tensor_tensor(result[:, kb, a:b], ds[kb, i], windows[kb][:, a:b], ADD)
+                queue.dma_start(out=out[kb * P : (kb + 1) * P, a:b], in_=result[:, kb, a:b])
 
         g_first = keep.tile([P, PACK, FIRST[1] - FIRST[0]], F32, name="g_edge")
         g_middle = keep.tile([P, PACK, MIDDLE[1] - MIDDLE[0]], F32, name="g_middle")
@@ -146,9 +147,9 @@ def tile_moe_bds_lin_none_kernel(tc, dyT, w_words, w_scales, gate, offs, out):
             scatter(kb, dx[:, kb, FIRST[0] : FIRST[1]], *FIRST)
         last_bank = psum.tile([P, KB, LAST[1] - LAST[0]], F32, name="last_bank")
         experts([last_bank[:, kb, :] for kb in range(KB)], *LAST)
-        for kb in range(KB):
-            nc.scalar.copy(out=dx[:, kb, MIDDLE[0] : MIDDLE[1]], in_=middle_banks[kb][:])
-            scatter(kb, dx[:, kb, MIDDLE[0] : MIDDLE[1]], *MIDDLE)
+        for kb, b in ((0, MIDDLE[1]), (1, HELD[0])):
+            nc.scalar.copy(out=dx[:, kb, MIDDLE[0] : b], in_=middle_banks[kb][:, 0 : b - MIDDLE[0]])
+            scatter(kb, dx[:, kb, MIDDLE[0] : b], MIDDLE[0], b)
 
         tail_bank = psum.tile([P, KB, TOKEN_BANKS[2][1] - TOKEN_BANKS[2][0]], F32, name="pair_bank")
         ds = {}
@@ -163,10 +164,18 @@ def tile_moe_bds_lin_none_kernel(tc, dyT, w_words, w_scales, gate, offs, out):
                     ds[kb, i] = psum.tile([P, BANK], F32, name="ds%d_%d" % (kb, i))[:]
                 else:
                     ds[kb, i] = tail_bank[:, kb, :]
+        for kb in range(KB):
+            for i, (a, b) in enumerate(TOKEN_BANKS):
                 product(ds[kb, i], E, kb, y_codes[:, a:b], y_scales[:, a:b])
 
-        dx_last = keep.tile([P, KB, LAST[1] - LAST[0]], F32, name="tokens%d" % TOKEN_LOADS[-1][0])
-        for kb in range(KB):
-            nc.scalar.copy(out=dx_last[:, kb, :], in_=last_bank[:, kb, :])
-            scatter(kb, dx_last[:, kb, :], *LAST)
-            combine(kb)
+        late = keep.tile([P, 3 * 256 + T], F32, name="tokens%d" % TOKEN_LOADS[-1][0])
+        nc.scalar.copy(out=late[:, 0:256], in_=last_bank[:, 0, :])
+        scatter(0, late[:, 0:256], *LAST)
+        nc.scalar.copy(out=late[:, 256:512], in_=middle_banks[1][:, HELD[0] - MIDDLE[0] : HELD[1] - MIDDLE[0]])
+        nc.scalar.copy(out=late[:, 512:768], in_=last_bank[:, 1, :])
+        scatter(1, late[:, 256:768], HELD[0], SLOTS)
+        for i, (a, b) in enumerate(TOKEN_BANKS):
+            nc.scalar.copy(out=late[:, 768 + a : 768 + b], in_=ds[0, i])
+            ds[0, i] = late[:, 768 + a : 768 + b]
+        combine(nc.gpsimd, nc.scalar, 0)
+        combine(nc.vector, nc.sync, 1)

@@ -119,18 +119,19 @@ def tile_moe_bds_lin_none_kernel(tc, dyT, w_words, w_scales, gate, offs, out):
         def scatter(kb, values, a, b):
             nc.vector.tensor_copy(windows[kb][:].indirect(offsets[:, a // 16 : b // 16]), values)
 
-        def combine(engine, queue, kb):
-            for i, (a, b) in enumerate(TOKEN_BANKS):
-                engine.tensor_tensor(result[:, kb, a:b], ds[kb, i], windows[kb][:, a:b], ADD)
-                queue.dma_start(out=out[kb * P : (kb + 1) * P, a:b], in_=result[:, kb, a:b])
+        def combine(engine, queue, kb, shared, a, b):
+            engine.tensor_tensor(result[:, kb, a:b], shared, windows[kb][:, a:b], ADD)
+            queue.dma_start(out=out[kb * P : (kb + 1) * P, a:b], in_=result[:, kb, a:b])
 
         g_first = keep.tile([P, PACK, FIRST[1] - FIRST[0]], F32, name="g_edge")
         g_middle = keep.tile([P, PACK, MIDDLE[1] - MIDDLE[0]], F32, name="g_middle")
         for t in range(PACK):
             gather(g_first, t, *FIRST)
             gather(g_middle, t, *MIDDLE)
-        interleave(g_bf[:, FIRST[0] : FIRST[1], :], g_first[:])
-        interleave(g_bf[:, MIDDLE[0] : MIDDLE[1], :], g_middle[:])
+        interleave(g_bf[:, FIRST[0] : FIRST[1], 0:3], g_first[:, 0:3, :])
+        nc.scalar.copy(out=g_bf[:, FIRST[0] : FIRST[1], 3], in_=g_first[:, 3, :])
+        for c0 in range(0, MIDDLE[1] - MIDDLE[0], 256):
+            interleave(g_bf[:, MIDDLE[0] + c0 : MIDDLE[0] + c0 + 256, :], g_middle[:, :, c0 : c0 + 256])
 
         first_bank = psum.tile([P, KB, FIRST[1] - FIRST[0]], F32, name="pair_bank")
         experts([first_bank[:, kb, :] for kb in range(KB)], *FIRST)
@@ -142,7 +143,8 @@ def tile_moe_bds_lin_none_kernel(tc, dyT, w_words, w_scales, gate, offs, out):
         interleave(g_bf[:, LAST[0] : LAST[1], :], g_last[:])
 
         middle_banks = [psum.tile([P, BANK], F32, name="middle_bank%d" % kb) for kb in range(KB)]
-        experts([bank[:] for bank in middle_banks], *MIDDLE)
+        for c0 in range(0, MIDDLE[1] - MIDDLE[0], 256):
+            experts([bank[:, c0 : c0 + 256] for bank in middle_banks], MIDDLE[0] + c0, MIDDLE[0] + c0 + 256)
         for kb in range(KB):
             scatter(kb, dx[:, kb, FIRST[0] : FIRST[1]], *FIRST)
         last_bank = psum.tile([P, KB, LAST[1] - LAST[0]], F32, name="last_bank")
@@ -158,7 +160,9 @@ def tile_moe_bds_lin_none_kernel(tc, dyT, w_words, w_scales, gate, offs, out):
                 j = [lo <= c0 < hi for lo, hi in TOKEN_LOADS].index(True)
                 lo = c0 - TOKEN_LOADS[j][0]
                 interleave(y_bf[:, c0 : c0 + COPY_TOKENS, :], tokens[j][:, :, lo : lo + COPY_TOKENS])
-            quantize(y_codes[:, a:b], y_scales[:, a:b], y_bf[:, a:b, :])
+            if i > 0:
+                lo = a if i == 2 else 0
+                quantize(y_codes[:, lo:b], y_scales[:, lo:b], y_bf[:, lo:b, :])
             for kb in range(KB):
                 if b - a == BANK:
                     ds[kb, i] = psum.tile([P, BANK], F32, name="ds%d_%d" % (kb, i))[:]
@@ -168,7 +172,7 @@ def tile_moe_bds_lin_none_kernel(tc, dyT, w_words, w_scales, gate, offs, out):
             for i, (a, b) in enumerate(TOKEN_BANKS):
                 product(ds[kb, i], E, kb, y_codes[:, a:b], y_scales[:, a:b])
 
-        late = keep.tile([P, 3 * 256 + T], F32, name="tokens%d" % TOKEN_LOADS[-1][0])
+        late = keep.tile([P, 4 * 256 + T], F32, name="tokens%d" % TOKEN_LOADS[-1][0])
         nc.scalar.copy(out=late[:, 0:256], in_=last_bank[:, 0, :])
         scatter(0, late[:, 0:256], *LAST)
         nc.scalar.copy(out=late[:, 256:512], in_=middle_banks[1][:, HELD[0] - MIDDLE[0] : HELD[1] - MIDDLE[0]])
@@ -177,5 +181,10 @@ def tile_moe_bds_lin_none_kernel(tc, dyT, w_words, w_scales, gate, offs, out):
         for i, (a, b) in enumerate(TOKEN_BANKS):
             nc.scalar.copy(out=late[:, 768 + a : 768 + b], in_=ds[0, i])
             ds[0, i] = late[:, 768 + a : 768 + b]
-        combine(nc.gpsimd, nc.scalar, 0)
-        combine(nc.vector, nc.sync, 1)
+        nc.scalar.copy(out=late[:, 768 + T : 1024 + T], in_=ds[1, 2])
+        for i, (a, b) in enumerate(TOKEN_BANKS):
+            combine(nc.gpsimd, nc.scalar, 0, ds[0, i], a, b)
+        combine(nc.gpsimd, nc.scalar, 1, late[:, 768 + T : 1024 + T], *TOKEN_BANKS[2])
+        combine(nc.vector, nc.sync, 1, ds[1, 0][:, 0:256], 0, 256)
+        combine(nc.vector, nc.sync, 1, ds[1, 0][:, 256:512], 256, 512)
+        combine(nc.vector, nc.sync, 1, ds[1, 1], 512, 1024)

@@ -22,12 +22,16 @@ P = 128
 PACK = 4
 KB = K // P
 BANK = 512
-FIRST, MIDDLE, LAST = (0, 256), (256, 768), (768, 1024)
-HELD = (512, 768)
-EARLY_EXPERTS = 2
-TOKEN_LOADS = [(0, 256), (256, 768), (768, 1280)]
-TOKEN_BANKS = [(0, 512), (512, 1024), (1024, 1280)]
-COPY_TOKENS = 256
+PIECE = 256
+LIST_ROWS = 16
+SCALE_ROWS = 4
+
+FIRST, MIDDLE, LAST = (0, PIECE), (PIECE, 3 * PIECE), (3 * PIECE, SLOTS)
+FIRST_EXPERTS = PIECE // C
+HELD = 2 * PIECE
+TOKEN_LOADS = [(0, PIECE), (PIECE, 3 * PIECE), (3 * PIECE, T)]
+TOKEN_QUANTIZE = [(0, 2 * BANK), (2 * BANK, T)]
+TOKEN_BANKS = [(0, BANK), (BANK, 2 * BANK), (2 * BANK, T)]
 
 
 def tile_moe_bds_lin_none_kernel(tc, dyT, w_words, w_scales, gate, offs, out):
@@ -37,11 +41,11 @@ def tile_moe_bds_lin_none_kernel(tc, dyT, w_words, w_scales, gate, offs, out):
         keep = ctx.enter_context(tc.tile_pool(name="keep", bufs=1))
         psum = ctx.enter_context(tc.psum_pool(name="psum", bufs=1))
 
-        offsets = keep.tile([P, SLOTS // 16], U16, name="offsets")
+        offsets = keep.tile([P, SLOTS // LIST_ROWS], U16, name="offsets")
         rows = [keep.tile([P, T], F32, name="rows%d" % t) for t in range(PACK)]
         gates = keep.tile([P, SLOTS], F32, name="gates")
         words = keep.tile([P, E + 1, 2 * K], U8, name="words", align_bytes=64)
-        planes = keep.tile([P, E + 1, K], U8, name="planes", align_bytes=64)
+        w_plane = keep.tile([P, E + 1, K], U8, name="w_plane", align_bytes=64)
         tokens = [keep.tile([P, PACK, b - a], F32, name="tokens%d" % a) for a, b in TOKEN_LOADS]
         windows = [keep.tile([P, T], F32, name="window%d" % kb) for kb in range(KB)]
         g_bf = keep.tile([P, SLOTS, PACK], BF16, name="g_bf", align_bytes=64)
@@ -55,9 +59,12 @@ def tile_moe_bds_lin_none_kernel(tc, dyT, w_words, w_scales, gate, offs, out):
 
         dy_rows = dyT.rearrange("(p t) c -> p t c", t=PACK)
 
-        nc.vector.memset(planes[:].bitcast(I32), 0)
+        nc.vector.memset(w_plane[:].bitcast(I32), 0)
         nc.vector.memset(windows[0][:], 0.0)
         nc.gpsimd.memset(windows[1][:], 0.0)
+
+        def load_gate(a, b):
+            nc.sync.dma_start(out=gates[:, a:b], in_=gate[0:P, a:b])
 
         def load_words(first, last):
             nc.sync.dma_start(
@@ -65,30 +72,26 @@ def tile_moe_bds_lin_none_kernel(tc, dyT, w_words, w_scales, gate, offs, out):
                 in_=w_words[first:last, 0].rearrange("e p b -> p e b").bitcast(I32),
             )
 
-        def load_gate(a, b):
-            nc.sync.dma_start(out=gates[:, a:b], in_=gate[0:P, a:b])
-
         nc.sync.dma_start(offsets[:], offs)
         load_gate(*FIRST)
         nc.sync.dma_start(out=rows[0][:], in_=dy_rows[:, 0, :])
         load_gate(*MIDDLE)
+        load_gate(*LAST)
         for t in range(1, PACK):
             nc.sync.dma_start(out=rows[t][:], in_=dy_rows[:, t, :])
-        load_gate(*LAST)
-        load_words(0, EARLY_EXPERTS)
-        for r in range(4):
+        load_words(0, FIRST_EXPERTS)
+        for r in range(SCALE_ROWS):
             nc.sync.dma_start(
-                out=planes[r:P:32, :, :].bitcast(I32),
-                in_=w_scales[:, 0, r:16:4, :].rearrange("e q k -> q e k").bitcast(I32),
+                out=w_plane[r:P:32, :, :].bitcast(I32),
+                in_=w_scales[:, 0, r : N // 32 : SCALE_ROWS, :].rearrange("e q k -> q e k").bitcast(I32),
             )
-        load_words(EARLY_EXPERTS, E + 1)
+        load_words(FIRST_EXPERTS, E + 1)
         for i, (a, b) in enumerate(TOKEN_LOADS):
             nc.sync.dma_start(out=tokens[i][:], in_=dy_rows[:, :, a:b])
 
-        def gather(g_rows, t, a, b):
-            nc.vector.tensor_tensor(
-                g_rows[:, t, :], rows[t][:].indirect(offsets[:, a // 16 : b // 16]), gates[:, a:b], MULT
-            )
+        def gather(g_row, t, a, b):
+            listed = offsets[:, a // LIST_ROWS : b // LIST_ROWS]
+            nc.vector.tensor_tensor(g_row, rows[t][:].indirect(listed), gates[:, a:b], MULT)
 
         def interleave(dst, src):
             nc.scalar.copy(
@@ -103,7 +106,7 @@ def tile_moe_bds_lin_none_kernel(tc, dyT, w_words, w_scales, gate, offs, out):
             nc.tensor.matmul_mx(
                 out=acc,
                 lhsT=words[:, e, 2 * P * kb : 2 * P * (kb + 1)].bitcast(FP4X4),
-                lhsT_scale=planes[:, e, P * kb : P * (kb + 1)],
+                lhsT_scale=w_plane[:, e, P * kb : P * (kb + 1)],
                 rhs=codes.bitcast(FP8X4),
                 rhs_scale=scales,
                 start=True,
@@ -117,74 +120,76 @@ def tile_moe_bds_lin_none_kernel(tc, dyT, w_words, w_scales, gate, offs, out):
                     product(sums[kb][:, c0 - a : c0 - a + C], c0 // C, kb, g_codes[:, c0 : c0 + C], g_scales[:, c0 : c0 + C])
 
         def scatter(kb, values, a, b):
-            nc.vector.tensor_copy(windows[kb][:].indirect(offsets[:, a // 16 : b // 16]), values)
+            listed = offsets[:, a // LIST_ROWS : b // LIST_ROWS]
+            nc.vector.tensor_copy(windows[kb][:].indirect(listed), values)
 
         def combine(engine, queue, kb, shared, a, b):
             engine.tensor_tensor(result[:, kb, a:b], shared, windows[kb][:, a:b], ADD)
             queue.dma_start(out=out[kb * P : (kb + 1) * P, a:b], in_=result[:, kb, a:b])
 
-        g_first = keep.tile([P, PACK, FIRST[1] - FIRST[0]], F32, name="g_edge")
-        g_middle = keep.tile([P, PACK, MIDDLE[1] - MIDDLE[0]], F32, name="g_middle")
+        g_first = keep.tile([P, PACK, PIECE], F32, name="g_edge")
+        g_middle = keep.tile([P, PACK, 2 * PIECE], F32, name="g_middle")
+        g_last_row0 = keep.tile([P, PIECE], F32, name="g_last_row0")
         for t in range(PACK):
-            gather(g_first, t, *FIRST)
-            gather(g_middle, t, *MIDDLE)
-        interleave(g_bf[:, FIRST[0] : FIRST[1], 0:3], g_first[:, 0:3, :])
-        nc.scalar.copy(out=g_bf[:, FIRST[0] : FIRST[1], 3], in_=g_first[:, 3, :])
-        for c0 in range(0, MIDDLE[1] - MIDDLE[0], 256):
-            interleave(g_bf[:, MIDDLE[0] + c0 : MIDDLE[0] + c0 + 256, :], g_middle[:, :, c0 : c0 + 256])
+            gather(g_first[:, t, :], t, *FIRST)
+            gather(g_middle[:, t, :], t, *MIDDLE)
+            if t == 0:
+                gather(g_last_row0[:], t, *LAST)
+                nc.scalar.copy(out=g_bf[:, LAST[0] : LAST[1], 0], in_=g_last_row0[:])
+        interleave(g_bf[:, FIRST[0] : FIRST[1], 0 : PACK - 1], g_first[:, 0 : PACK - 1, :])
+        nc.scalar.copy(out=g_bf[:, FIRST[0] : FIRST[1], PACK - 1], in_=g_first[:, PACK - 1, :])
+        for c0 in range(0, 2 * PIECE, PIECE):
+            interleave(g_bf[:, MIDDLE[0] + c0 : MIDDLE[0] + c0 + PIECE, :], g_middle[:, :, c0 : c0 + PIECE])
 
-        first_bank = psum.tile([P, KB, FIRST[1] - FIRST[0]], F32, name="pair_bank")
+        first_bank = psum.tile([P, KB, PIECE], F32, name="pair_bank")
         experts([first_bank[:, kb, :] for kb in range(KB)], *FIRST)
         nc.scalar.copy(out=dx[:, :, FIRST[0] : FIRST[1]], in_=first_bank[:])
 
-        g_last = keep.tile([P, PACK, LAST[1] - LAST[0]], F32, name="g_edge")
-        for t in range(PACK):
-            gather(g_last, t, *LAST)
-        interleave(g_bf[:, LAST[0] : LAST[1], :], g_last[:])
+        g_last = keep.tile([P, PACK - 1, PIECE], F32, name="g_edge")
+        for t in range(1, PACK):
+            gather(g_last[:, t - 1, :], t, *LAST)
+        interleave(g_bf[:, LAST[0] : LAST[1], 1:PACK], g_last[:])
 
         middle_banks = [psum.tile([P, BANK], F32, name="middle_bank%d" % kb) for kb in range(KB)]
-        for c0 in range(0, MIDDLE[1] - MIDDLE[0], 256):
-            experts([bank[:, c0 : c0 + 256] for bank in middle_banks], MIDDLE[0] + c0, MIDDLE[0] + c0 + 256)
+        for c0 in range(0, 2 * PIECE, PIECE):
+            experts([bank[:, c0 : c0 + PIECE] for bank in middle_banks], MIDDLE[0] + c0, MIDDLE[0] + c0 + PIECE)
         for kb in range(KB):
             scatter(kb, dx[:, kb, FIRST[0] : FIRST[1]], *FIRST)
-        last_bank = psum.tile([P, KB, LAST[1] - LAST[0]], F32, name="last_bank")
+        last_bank = psum.tile([P, KB, PIECE], F32, name="last_bank")
         experts([last_bank[:, kb, :] for kb in range(KB)], *LAST)
-        for kb, b in ((0, MIDDLE[1]), (1, HELD[0])):
-            nc.scalar.copy(out=dx[:, kb, MIDDLE[0] : b], in_=middle_banks[kb][:, 0 : b - MIDDLE[0]])
-            scatter(kb, dx[:, kb, MIDDLE[0] : b], MIDDLE[0], b)
+        for kb, end in ((0, MIDDLE[1]), (1, HELD)):
+            nc.scalar.copy(out=dx[:, kb, MIDDLE[0] : end], in_=middle_banks[kb][:, 0 : end - MIDDLE[0]])
+            scatter(kb, dx[:, kb, MIDDLE[0] : end], MIDDLE[0], end)
 
-        tail_bank = psum.tile([P, KB, TOKEN_BANKS[2][1] - TOKEN_BANKS[2][0]], F32, name="pair_bank")
-        ds = {}
-        for i, (a, b) in enumerate(TOKEN_BANKS):
-            for c0 in range(a, b, COPY_TOKENS):
-                j = [lo <= c0 < hi for lo, hi in TOKEN_LOADS].index(True)
-                lo = c0 - TOKEN_LOADS[j][0]
-                interleave(y_bf[:, c0 : c0 + COPY_TOKENS, :], tokens[j][:, :, lo : lo + COPY_TOKENS])
-            if i > 0:
-                lo = a if i == 2 else 0
-                quantize(y_codes[:, lo:b], y_scales[:, lo:b], y_bf[:, lo:b, :])
-            for kb in range(KB):
-                if b - a == BANK:
-                    ds[kb, i] = psum.tile([P, BANK], F32, name="ds%d_%d" % (kb, i))[:]
-                else:
-                    ds[kb, i] = tail_bank[:, kb, :]
+        tail_bank = psum.tile([P, KB, T - 2 * BANK], F32, name="pair_bank")
+        ds = [[psum.tile([P, BANK], F32, name="ds%d_%d" % (kb, i))[:] for i in range(2)] + [tail_bank[:, kb, :]] for kb in range(KB)]
+        for a, b in TOKEN_QUANTIZE:
+            for c0 in range(a, b, PIECE):
+                i = [lo <= c0 < hi for lo, hi in TOKEN_LOADS].index(True)
+                lo = c0 - TOKEN_LOADS[i][0]
+                interleave(y_bf[:, c0 : c0 + PIECE, :], tokens[i][:, :, lo : lo + PIECE])
+            quantize(y_codes[:, a:b], y_scales[:, a:b], y_bf[:, a:b, :])
         for kb in range(KB):
             for i, (a, b) in enumerate(TOKEN_BANKS):
-                product(ds[kb, i], E, kb, y_codes[:, a:b], y_scales[:, a:b])
+                product(ds[kb][i], E, kb, y_codes[:, a:b], y_scales[:, a:b])
 
-        late = keep.tile([P, 4 * 256 + T], F32, name="tokens%d" % TOKEN_LOADS[-1][0])
-        nc.scalar.copy(out=late[:, 0:256], in_=last_bank[:, 0, :])
-        scatter(0, late[:, 0:256], *LAST)
-        nc.scalar.copy(out=late[:, 256:512], in_=middle_banks[1][:, HELD[0] - MIDDLE[0] : HELD[1] - MIDDLE[0]])
-        nc.scalar.copy(out=late[:, 512:768], in_=last_bank[:, 1, :])
-        scatter(1, late[:, 256:768], HELD[0], SLOTS)
+        late = keep.tile([P, PIECE + (SLOTS - HELD) + T + PIECE], F32, name="tokens%d" % TOKEN_LOADS[-1][0])
+        dx0_late = late[:, 0:PIECE]
+        dx1_late = late[:, PIECE : PIECE + SLOTS - HELD]
+        ds0_staged = late[:, PIECE + SLOTS - HELD : PIECE + SLOTS - HELD + T]
+        ds1_tail = late[:, PIECE + SLOTS - HELD + T :]
+        nc.scalar.copy(out=dx0_late, in_=last_bank[:, 0, :])
+        scatter(0, dx0_late, *LAST)
+        nc.scalar.copy(out=dx1_late[:, 0 : LAST[0] - HELD], in_=middle_banks[1][:, HELD - MIDDLE[0] :])
+        nc.scalar.copy(out=dx1_late[:, LAST[0] - HELD :], in_=last_bank[:, 1, :])
+        scatter(1, dx1_late, HELD, SLOTS)
         for i, (a, b) in enumerate(TOKEN_BANKS):
-            nc.scalar.copy(out=late[:, 768 + a : 768 + b], in_=ds[0, i])
-            ds[0, i] = late[:, 768 + a : 768 + b]
-        nc.scalar.copy(out=late[:, 768 + T : 1024 + T], in_=ds[1, 2])
-        for i, (a, b) in enumerate(TOKEN_BANKS):
-            combine(nc.gpsimd, nc.scalar, 0, ds[0, i], a, b)
-        combine(nc.gpsimd, nc.scalar, 1, late[:, 768 + T : 1024 + T], *TOKEN_BANKS[2])
-        combine(nc.vector, nc.sync, 1, ds[1, 0][:, 0:256], 0, 256)
-        combine(nc.vector, nc.sync, 1, ds[1, 0][:, 256:512], 256, 512)
-        combine(nc.vector, nc.sync, 1, ds[1, 1], 512, 1024)
+            nc.scalar.copy(out=ds0_staged[:, a:b], in_=ds[0][i])
+        nc.scalar.copy(out=ds1_tail, in_=ds[1][2])
+
+        for a, b in TOKEN_BANKS:
+            combine(nc.gpsimd, nc.scalar, 0, ds0_staged[:, a:b], a, b)
+        combine(nc.gpsimd, nc.scalar, 1, ds1_tail, *TOKEN_BANKS[2])
+        combine(nc.vector, nc.sync, 1, ds[1][0][:, 0:PIECE], 0, PIECE)
+        combine(nc.vector, nc.sync, 1, ds[1][0][:, PIECE:BANK], PIECE, BANK)
+        combine(nc.vector, nc.sync, 1, ds[1][1], *TOKEN_BANKS[1])

from contextlib import ExitStack

import concourse.mybir as mybir

K, T, E, C, N = 256, 1280, 8, 128, 512
SLOTS = E * C
FLOPS = 2 * N * K * (SLOTS + T)
BYTES = 4 * N * T + (E + 1) * (N * K // 2 + N * K // 32) + 4 * SLOTS + 2 * SLOTS + 4 * K * T

F32 = mybir.dt.float32
BF16 = mybir.dt.bfloat16
I32 = mybir.dt.int32
U32 = mybir.dt.uint32
U16 = mybir.dt.uint16
U8 = mybir.dt.uint8
FP8X4 = mybir.dt.float8_e4m3fn_x4
FP4X4 = mybir.dt.float4_e2m1fn_x4
MULT = mybir.AluOpType.mult
ADD = mybir.AluOpType.add

P = 128
PACK = 4
KB = K // P
BANK = 512
PIECE = 256
LIST_ROWS = 16
SCALE_ROWS = 4

FIRST, MIDDLE, LAST = (0, PIECE), (PIECE, 3 * PIECE), (3 * PIECE, SLOTS)
FIRST_EXPERTS = PIECE // C
HELD = 2 * PIECE
TOKEN_LOADS = [(0, PIECE), (PIECE, 3 * PIECE), (3 * PIECE, T)]
TOKEN_QUANTIZE = [(0, 2 * BANK), (2 * BANK, T)]
TOKEN_BANKS = [(0, BANK), (BANK, 2 * BANK), (2 * BANK, T)]


def tile_moe_bds_lin_none_kernel(tc, dyT, w_words, w_scales, gate, offs, out):
    nc = tc.nc

    with ExitStack() as ctx:
        keep = ctx.enter_context(tc.tile_pool(name="keep", bufs=1))
        psum = ctx.enter_context(tc.psum_pool(name="psum", bufs=1))

        offsets = keep.tile([P, SLOTS // LIST_ROWS], U16, name="offsets")
        rows = [keep.tile([P, T], F32, name="rows%d" % t) for t in range(PACK)]
        gates = keep.tile([P, SLOTS], F32, name="gates")
        words = keep.tile([P, E + 1, 2 * K], U8, name="words", align_bytes=64)
        w_plane = keep.tile([P, E + 1, K], U8, name="w_plane", align_bytes=64)
        tokens = [keep.tile([P, PACK, b - a], F32, name="tokens%d" % a) for a, b in TOKEN_LOADS]
        windows = [keep.tile([P, T], F32, name="window%d" % kb) for kb in range(KB)]
        g_bf = keep.tile([P, SLOTS, PACK], BF16, name="g_bf", align_bytes=64)
        g_codes = keep.tile([P, SLOTS], U32, name="g_codes", align_bytes=64)
        g_scales = keep.tile([P, SLOTS], U8, name="g_scales", align_bytes=64)
        y_bf = keep.tile([P, T, PACK], BF16, name="y_bf", align_bytes=64)
        y_codes = keep.tile([P, T], U32, name="y_codes", align_bytes=64)
        y_scales = keep.tile([P, T], U8, name="y_scales", align_bytes=64)
        dx = keep.tile([P, KB, MIDDLE[1]], F32, name="dx")
        result = keep.tile([P, KB, T], F32, name="result")

        dy_rows = dyT.rearrange("(p t) c -> p t c", t=PACK)

        nc.vector.memset(w_plane[:].bitcast(I32), 0)
        nc.vector.memset(windows[0][:], 0.0)
        nc.gpsimd.memset(windows[1][:], 0.0)

        def load_gate(a, b):
            nc.sync.dma_start(out=gates[:, a:b], in_=gate[0:P, a:b])

        def load_words(first, last):
            nc.sync.dma_start(
                out=words[:, first:last, :].bitcast(I32),
                in_=w_words[first:last, 0].rearrange("e p b -> p e b").bitcast(I32),
            )

        nc.sync.dma_start(offsets[:], offs)
        load_gate(*FIRST)
        nc.sync.dma_start(out=rows[0][:], in_=dy_rows[:, 0, :])
        load_gate(*MIDDLE)
        load_gate(*LAST)
        for t in range(1, PACK):
            nc.sync.dma_start(out=rows[t][:], in_=dy_rows[:, t, :])
        load_words(0, FIRST_EXPERTS)
        for r in range(SCALE_ROWS):
            nc.sync.dma_start(
                out=w_plane[r:P:32, :, :].bitcast(I32),
                in_=w_scales[:, 0, r : N // 32 : SCALE_ROWS, :].rearrange("e q k -> q e k").bitcast(I32),
            )
        load_words(FIRST_EXPERTS, E + 1)
        for i, (a, b) in enumerate(TOKEN_LOADS):
            nc.sync.dma_start(out=tokens[i][:], in_=dy_rows[:, :, a:b])

        def gather(g_row, t, a, b):
            listed = offsets[:, a // LIST_ROWS : b // LIST_ROWS]
            nc.vector.tensor_tensor(g_row, rows[t][:].indirect(listed), gates[:, a:b], MULT)

        def interleave(dst, src):
            nc.scalar.copy(
                out=dst.rearrange("p (c i) t -> p c t i", i=4),
                in_=src.rearrange("p t (c i) -> p c t i", i=4),
            )

        def quantize(codes, scales, values):
            nc.vector.quantize_mx(out=codes.bitcast(FP8X4), scales=scales, in_=values.rearrange("p c t -> p (c t)"))

        def product(acc, e, kb, codes, scales):
            nc.tensor.matmul_mx(
                out=acc,
                lhsT=words[:, e, 2 * P * kb : 2 * P * (kb + 1)].bitcast(FP4X4),
                lhsT_scale=w_plane[:, e, P * kb : P * (kb + 1)],
                rhs=codes.bitcast(FP8X4),
                rhs_scale=scales,
                start=True,
                stop=True,
            )

        def experts(sums, a, b):
            quantize(g_codes[:, a:b], g_scales[:, a:b], g_bf[:, a:b, :])
            for kb in range(KB):
                for c0 in range(a, b, C):
                    product(sums[kb][:, c0 - a : c0 - a + C], c0 // C, kb, g_codes[:, c0 : c0 + C], g_scales[:, c0 : c0 + C])

        def scatter(kb, values, a, b):
            listed = offsets[:, a // LIST_ROWS : b // LIST_ROWS]
            nc.vector.tensor_copy(windows[kb][:].indirect(listed), values)

        def combine(engine, queue, kb, shared, a, b):
            engine.tensor_tensor(result[:, kb, a:b], shared, windows[kb][:, a:b], ADD)
            queue.dma_start(out=out[kb * P : (kb + 1) * P, a:b], in_=result[:, kb, a:b])

        g_first = keep.tile([P, PACK, PIECE], F32, name="g_edge")
        g_middle = keep.tile([P, PACK, 2 * PIECE], F32, name="g_middle")
        g_last_row0 = keep.tile([P, PIECE], F32, name="g_last_row0")
        for t in range(PACK):
            gather(g_first[:, t, :], t, *FIRST)
            gather(g_middle[:, t, :], t, *MIDDLE)
            if t == 0:
                gather(g_last_row0[:], t, *LAST)
                nc.scalar.copy(out=g_bf[:, LAST[0] : LAST[1], 0], in_=g_last_row0[:])
        interleave(g_bf[:, FIRST[0] : FIRST[1], 0 : PACK - 1], g_first[:, 0 : PACK - 1, :])
        nc.scalar.copy(out=g_bf[:, FIRST[0] : FIRST[1], PACK - 1], in_=g_first[:, PACK - 1, :])
        for c0 in range(0, 2 * PIECE, PIECE):
            interleave(g_bf[:, MIDDLE[0] + c0 : MIDDLE[0] + c0 + PIECE, :], g_middle[:, :, c0 : c0 + PIECE])

        first_bank = psum.tile([P, KB, PIECE], F32, name="pair_bank")
        experts([first_bank[:, kb, :] for kb in range(KB)], *FIRST)
        nc.scalar.copy(out=dx[:, :, FIRST[0] : FIRST[1]], in_=first_bank[:])

        g_last = keep.tile([P, PACK - 1, PIECE], F32, name="g_edge")
        for t in range(1, PACK):
            gather(g_last[:, t - 1, :], t, *LAST)
        interleave(g_bf[:, LAST[0] : LAST[1], 1:PACK], g_last[:])

        middle_banks = [psum.tile([P, BANK], F32, name="middle_bank%d" % kb) for kb in range(KB)]
        for c0 in range(0, 2 * PIECE, PIECE):
            experts([bank[:, c0 : c0 + PIECE] for bank in middle_banks], MIDDLE[0] + c0, MIDDLE[0] + c0 + PIECE)
        for kb in range(KB):
            scatter(kb, dx[:, kb, FIRST[0] : FIRST[1]], *FIRST)
        last_bank = psum.tile([P, KB, PIECE], F32, name="last_bank")
        experts([last_bank[:, kb, :] for kb in range(KB)], *LAST)
        for kb, end in ((0, MIDDLE[1]), (1, HELD)):
            nc.scalar.copy(out=dx[:, kb, MIDDLE[0] : end], in_=middle_banks[kb][:, 0 : end - MIDDLE[0]])
            scatter(kb, dx[:, kb, MIDDLE[0] : end], MIDDLE[0], end)

        tail_bank = psum.tile([P, KB, T - 2 * BANK], F32, name="pair_bank")
        ds = [[psum.tile([P, BANK], F32, name="ds%d_%d" % (kb, i))[:] for i in range(2)] + [tail_bank[:, kb, :]] for kb in range(KB)]
        for a, b in TOKEN_QUANTIZE:
            for c0 in range(a, b, PIECE):
                i = [lo <= c0 < hi for lo, hi in TOKEN_LOADS].index(True)
                lo = c0 - TOKEN_LOADS[i][0]
                interleave(y_bf[:, c0 : c0 + PIECE, :], tokens[i][:, :, lo : lo + PIECE])
            quantize(y_codes[:, a:b], y_scales[:, a:b], y_bf[:, a:b, :])
        for kb in range(KB):
            for i, (a, b) in enumerate(TOKEN_BANKS):
                product(ds[kb][i], E, kb, y_codes[:, a:b], y_scales[:, a:b])

        late = keep.tile([P, PIECE + (SLOTS - HELD) + T + PIECE], F32, name="tokens%d" % TOKEN_LOADS[-1][0])
        dx0_late = late[:, 0:PIECE]
        dx1_late = late[:, PIECE : PIECE + SLOTS - HELD]
        ds0_staged = late[:, PIECE + SLOTS - HELD : PIECE + SLOTS - HELD + T]
        ds1_tail = late[:, PIECE + SLOTS - HELD + T :]
        nc.scalar.copy(out=dx0_late, in_=last_bank[:, 0, :])
        scatter(0, dx0_late, *LAST)
        nc.scalar.copy(out=dx1_late[:, 0 : LAST[0] - HELD], in_=middle_banks[1][:, HELD - MIDDLE[0] :])
        nc.scalar.copy(out=dx1_late[:, LAST[0] - HELD :], in_=last_bank[:, 1, :])
        scatter(1, dx1_late, HELD, SLOTS)
        for i, (a, b) in enumerate(TOKEN_BANKS):
            nc.scalar.copy(out=ds0_staged[:, a:b], in_=ds[0][i])
        nc.scalar.copy(out=ds1_tail, in_=ds[1][2])

        for a, b in TOKEN_BANKS:
            combine(nc.gpsimd, nc.scalar, 0, ds0_staged[:, a:b], a, b)
        combine(nc.gpsimd, nc.scalar, 1, ds1_tail, *TOKEN_BANKS[2])
        combine(nc.vector, nc.sync, 1, ds[1][0][:, 0:PIECE], 0, PIECE)
        combine(nc.vector, nc.sync, 1, ds[1][0][:, PIECE:BANK], PIECE, BANK)
        combine(nc.vector, nc.sync, 1, ds[1][1], *TOKEN_BANKS[1])
